import numpy as np
import ml_dtypes


def mxq(x, axis, fmt="e4m3"):
    dtype, down = {"e4m3": (ml_dtypes.float8_e4m3fn, 7), "e5m2": (ml_dtypes.float8_e5m2, 14)}[fmt]
    v = np.moveaxis(np.asarray(x, np.float32).astype(ml_dtypes.bfloat16).astype(np.float64), axis, -1)
    blocks = v.reshape(v.shape[:-1] + (-1, 32))
    amax = np.abs(blocks).max(-1, keepdims=True)
    byte = np.maximum(np.where(amax > 0, np.frexp(amax)[1] - 1 + 127, 0) - down, 1)
    scale = np.exp2(byte - 127.0)
    codes = (blocks / scale).astype(np.float32).astype(dtype).astype(np.float64)
    return np.moveaxis((codes * scale).reshape(v.shape), -1, axis)


WIDE = False


def mx_kscale(k, group=512):
    if not WIDE:
        return np.ones(k)
    levels = np.array([10, -10, 5, -5, 0])
    if group != 512:
        return np.exp2(np.random.permutation(np.resize(levels, k // group))).repeat(group)
    if k % 512:
        return np.exp2(np.random.permutation(np.resize(levels, k // 32))).repeat(32)
    a = np.empty((k // 512, 16))
    for p in range(k // 512):
        a[p, :8] = np.random.permutation(np.resize(levels, 8))
        for g in range(8):
            far = levels[np.abs(levels - a[p, g]) >= 10]
            a[p, g + 8] = far[np.random.randint(len(far))]
    return np.exp2(a.ravel()).repeat(32)


def f64(x):
    return np.asarray(x).astype(np.float64)


def striped(idx):
    return np.tile(np.asarray(idx).reshape(-1, 16).T, (8, 1)).astype(np.uint16)


def unstriped(offs):
    return offs[:16].T.reshape(-1).astype(np.int64)


H, KV, D, NQ, N = 2, 2, 256, 512, 512


def setup_inputs():
    n = np.random.standard_normal
    s = mx_kscale(D, 0)[:, None]
    u = mx_kscale(N)
    t = np.random.uniform(0.5, 2.0, N) * u
    v = n((KV, N, 128))
    v[:, :, 127] = 1.0
    return {
        "qT": (n((H, D, NQ)) * s * (0.70 / np.sqrt(D))).astype(np.float32),
        "kT": (n((KV, D, N)) / s).astype(np.float32),
        "t": t.reshape(N, 1).astype(np.float32),
        "v": (v / t[:, None]).astype(np.float32),
        "kb": (0.5 * n((N, 1))).astype(np.float32),
        "mask": (np.arange(N)[:, None] <= np.sort(np.random.randint(N // 4, N, NQ))[None, :]).astype(np.float32),
    }


def reference(qT, kT, t, v, kb, mask):
    a = mxq(f64(kT), 1, "e4m3").transpose(0, 2, 1) @ mxq(f64(qT), 1, "e4m3")
    a = a + f64(kb)
    p = np.square(np.maximum(a, 0.0))
    p = p * f64(mask)
    w = p * f64(t)
    y = mxq(w, 1, "e4m3").transpose(0, 2, 1) @ mxq(f64(v), 1, "e4m3")
    y = y / (y[:, :, 127:128] + 1.0)
    return y

@@ -1,0 +1,268 @@
+from contextlib import ExitStack
+
+import concourse.mybir as mybir
+
+H, D, NQ, N, E = 2, 256, 512, 512, 128
+FLOPS = 2 * H * N * NQ * D + 2 * H * NQ * N * E
+
+F32 = mybir.dt.float32
+BF16 = mybir.dt.bfloat16
+U32 = mybir.dt.uint32
+U8 = mybir.dt.uint8
+FP8X4 = mybir.dt.float8_e4m3fn_x4
+ACT = mybir.ActivationFunctionType
+ALU = mybir.AluOpType
+
+P = 128
+PACK = 4
+ROWS = D // PACK
+HALF = NQ // 2
+QT = 128
+SCORE_BANKS = 3
+K_SPLIT = 88
+Q_SPLIT = 176
+
+
+def tile_rows_a_relu2_kb_mask_kernel(tc, qT, kT, t, v, kb, mask, out):
+    nc = tc.nc
+    with ExitStack() as ctx:
+        sb = ctx.enter_context(tc.tile_pool(name="sb", bufs=1))
+        ps = ctx.enter_context(tc.psum_pool(name="ps", bufs=1))
+        ctx.enter_context(tc.manual_schedule())
+
+        def tile(name, shape, dtype):
+            return sb.tile(shape, dtype, name=name, align_bytes=64)
+
+        t_sb = tile("t_sb", [P, PACK], F32)
+        kb_sb = tile("kb_sb", [P, PACK], F32)
+        k_raw = tile("k_raw", [P, PACK, N], F32)
+        q_raw = [tile("q_raw%d" % u, [P, PACK, HALF], F32) for u in range(2)]
+        m_raw = [tile("m_raw%d" % u, [P, PACK, HALF], F32) for u in range(2)]
+        v_raw = tile("v_raw", [P, H, PACK * E], F32)
+
+        nc.scalar.dma_start(out=t_sb[:], in_=t.rearrange("(p r) o -> p (r o)", r=PACK))
+        nc.scalar.dma_start(out=kb_sb[:], in_=kb.rearrange("(p r) o -> p (r o)", r=PACK))
+        q_rows = qT.rearrange("h (p j) n -> (h p) j n", j=PACK)
+        m_rows = mask.rearrange("(p r) n -> p r n", r=PACK)
+        nc.sync.dma_start(out=k_raw[:], in_=kT.rearrange("h (p j) n -> (h p) j n", j=PACK))
+        nc.sync.dma_start(out=q_raw[0][:], in_=q_rows[:, :, 0:HALF])
+        nc.sync.dma_start(out=q_raw[1][:], in_=q_rows[:, :, HALF:NQ])
+        nc.sync.dma_start(out=m_raw[0][:], in_=m_rows[:, :, 0:HALF])
+        nc.sync.dma_start(out=v_raw[:], in_=v.rearrange("h (p j) e -> p h (j e)", j=PACK))
+        nc.sync.dma_start(out=m_raw[1][:], in_=m_rows[:, :, HALF:NQ])
+
+        t_sign = tile("t_sign", [P, PACK], F32)
+        t_abs = tile("t_abs", [P, PACK], F32)
+        half_root = tile("half_root", [P, PACK], F32)
+        inv_half_root = tile("inv_half_root", [P, PACK], F32)
+        newton = tile("newton", [P, PACK], F32)
+        root = tile("root", [P, PACK], F32)
+        kb_root = tile("kb_root", [P, PACK], F32)
+        nc.vector.scalar_tensor_tensor(
+            out=t_abs[:], in0=t_sb[:], scalar=-1.0, in1=t_sb[:], op0=ALU.mult, op1=ALU.max
+        )
+        nc.scalar.activation(out=half_root[:], in_=t_abs[:], func=ACT.Sqrt, scale=0.25)
+        nc.scalar.activation(out=t_sign[:], in_=t_sb[:], func=ACT.Sign)
+        nc.vector.reciprocal(out=inv_half_root[:], in_=half_root[:])
+        nc.vector.scalar_tensor_tensor(
+            out=newton[:], in0=t_abs[:], scalar=0.25, in1=inv_half_root[:], op0=ALU.mult, op1=ALU.mult
+        )
+
+        k_bf = tile("k_bf", [P, PACK, P * PACK], BF16)
+        k_codes = tile("k_codes", [P, N], U32)
+        k_scales = tile("k_scales", [P, N], U8)
+        k_src = k_raw[:].rearrange("p j (m r) -> p m j r", r=PACK)
+        k_dst = k_bf[:].rearrange("p r (m j) -> p m j r", j=PACK)
+        nc.vector.tensor_copy(out=k_dst[:, 0:K_SPLIT], in_=k_src[:, 0:K_SPLIT])
+        nc.scalar.copy(out=k_dst[:, K_SPLIT:P], in_=k_src[:, K_SPLIT:P])
+        nc.vector.tensor_tensor(out=root[:], in0=newton[:], in1=half_root[:], op=ALU.add)
+        nc.vector.quantize_mx(
+            out=k_codes[:].bitcast(FP8X4), scales=k_scales[:], in_=k_bf[:].rearrange("p r n -> p (r n)")
+        )
+        nc.vector.tensor_tensor(out=kb_root[:], in0=kb_sb[:], in1=root[:], op=ALU.mult)
+
+        def by_fours(raw, packed):
+            src = raw.rearrange("p j (c i) -> p c j i", i=PACK)
+            dst = packed.rearrange("p (c i j) -> p c j i", i=PACK, j=PACK)
+            return src, dst
+
+        q_bf = [tile("q_bf%d" % u, [P, HALF * PACK], BF16) for u in range(2)]
+        q_codes = [tile("q_codes%d" % u, [P, HALF], U32) for u in range(2)]
+        q_scales = [tile("q_scales%d" % u, [P, HALF], U8) for u in range(2)]
+        m_bf = [tile("m_bf%d" % u, [P, HALF * PACK], BF16) for u in range(2)]
+        v_bf = tile("v_bf", [P, H, E * PACK], BF16)
+        v_codes = tile("v_codes", [P, H * E], U32)
+        v_scales = tile("v_scales", [P, H * E], U8)
+
+        def quantize(codes, scales, packed):
+            nc.vector.quantize_mx(out=codes.bitcast(FP8X4), scales=scales, in_=packed)
+
+        score_banks = [[ps.tile([P, HALF], F32, name="score%d_%d" % (h, b)) for b in range(SCORE_BANKS)] for h in range(H)]
+        y_banks = [ps.tile([P, 2 * HALF], F32, name="y%d" % b) for b in range(2)]
+        relu = {}
+        w_sq = {}
+        w_bf = {}
+        w_codes = {}
+        w_scales = {}
+        den = {}
+        inv = {}
+        res = {}
+        for u in range(2):
+            for h in range(H):
+                s = "%d%d" % (h, u)
+                relu[h, u] = tile("relu" + s, [P, PACK, HALF], F32)
+                w_sq[h, u] = tile("w_sq" + s, [P, HALF * PACK], BF16)
+                w_bf[h, u] = tile("w_bf" + s, [P, HALF * PACK], BF16)
+                w_codes[h, u] = tile("w_codes" + s, [P, HALF], U32)
+                w_scales[h, u] = tile("w_scales" + s, [P, HALF], U8)
+                den[h, u] = tile("den" + s, [P, 2], F32)
+                inv[h, u] = tile("inv" + s, [P, 2], F32)
+                res[h, u] = tile("res" + s, [P, 2, E], F32)
+
+        def scores(h, u, r):
+            bank = score_banks[h][(PACK * u + r) % SCORE_BANKS]
+            rows = slice(ROWS * h, ROWS * (h + 1))
+            toks = slice(P * r, P * (r + 1))
+            for c in range(2):
+                cols = slice(QT * c, QT * (c + 1))
+                nc.tensor.matmul_mx(
+                    out=bank[:, cols],
+                    lhsT=k_codes[rows, toks].bitcast(FP8X4),
+                    lhsT_scale=k_scales[rows, toks],
+                    rhs=q_codes[u][rows, cols].bitcast(FP8X4),
+                    rhs_scale=q_scales[u][rows, cols],
+                    start=True,
+                    stop=True,
+                )
+
+        def rectify(h, u, r):
+            bank = score_banks[h][(PACK * u + r) % SCORE_BANKS]
+            nc.scalar.activation(
+                out=relu[h, u][:, r, :], in_=bank[:], func=ACT.Relu, scale=root[:, r : r + 1], bias=kb_root[:, r : r + 1]
+            )
+
+        def square_scalar(h, u):
+            src, dst = by_fours(relu[h, u][:], w_sq[h, u][:])
+            nc.scalar.activation(out=dst, in_=src, func=ACT.Square)
+
+        def square_vector(h, u):
+            src, dst = by_fours(relu[h, u][:], w_sq[h, u][:])
+            nc.vector.tensor_tensor(out=dst, in0=src, in1=src, op=ALU.mult)
+
+        def apply_mask(h, u):
+            nc.vector.tensor_tensor(out=w_bf[h, u][:], in0=w_sq[h, u][:], in1=m_bf[u][:], op=ALU.mult)
+
+        def quantize_w(h, u):
+            quantize(w_codes[h, u][:], w_scales[h, u][:], w_bf[h, u][:])
+
+        def values(h, u):
+            for c in range(2):
+                cols = slice(QT * c, QT * (c + 1))
+                feats = slice(E * h, E * (h + 1))
+                nc.tensor.matmul_mx(
+                    out=y_banks[h][:, HALF * u + E * c : HALF * u + E * (c + 1)],
+                    lhsT=w_codes[h, u][:, cols].bitcast(FP8X4),
+                    lhsT_scale=w_scales[h, u][:, cols],
+                    rhs=v_codes[:, feats].bitcast(FP8X4),
+                    rhs_scale=v_scales[:, feats],
+                    start=True,
+                    stop=True,
+                )
+
+        def y_view(h, u):
+            return y_banks[h][:, HALF * u : HALF * (u + 1)].rearrange("p (c e) -> p c e", c=2)
+
+        def denominator(h, u):
+            nc.vector.tensor_scalar(
+                out=den[h, u][:], in0=y_view(h, u)[:, :, E - 1], scalar1=1.0, scalar2=None, op0=ALU.add
+            )
+
+        def invert(h, u):
+            nc.vector.reciprocal(out=inv[h, u][:], in_=den[h, u][:])
+
+        def finish(h, u):
+            for c in range(2):
+                nc.scalar.activation(
+                    out=res[h, u][:, c, :], in_=y_view(h, u)[:, c, :], func=ACT.Copy, scale=inv[h, u][:, c : c + 1]
+                )
+            nc.sync.dma_start(
+                out=out[h, HALF * u : HALF * (u + 1), :].rearrange("(c p) e -> p c e", p=P), in_=res[h, u][:]
+            )
+
+        def pack_values(h):
+            src, dst = by_fours(v_raw[:, h, :].rearrange("p (j e) -> p j e", j=PACK), v_bf[:, h, :])
+            sign = t_sign[:].unsqueeze(1).unsqueeze(3).to_broadcast([P, E // PACK, PACK, PACK])
+            nc.vector.tensor_tensor(out=dst, in0=src, in1=sign, op=ALU.mult)
+
+        def pack_vector(raw, packed):
+            src, dst = by_fours(raw[:], packed[:])
+            nc.vector.tensor_copy(out=dst, in_=src)
+
+        src, dst = by_fours(q_raw[0][:], q_bf[0][:])
+        nc.vector.tensor_copy(out=dst[:, 0 : Q_SPLIT // PACK], in_=src[:, 0 : Q_SPLIT // PACK])
+        nc.scalar.copy(out=dst[:, Q_SPLIT // PACK :], in_=src[:, Q_SPLIT // PACK :])
+        quantize(q_codes[0][:], q_scales[0][:], q_bf[0][:])
+        pack_vector(q_raw[1], q_bf[1])
+        for r in range(3):
+            scores(0, 0, r)
+        scores(1, 0, 0)
+        quantize(q_codes[1][:], q_scales[1][:], q_bf[1][:])
+        pack_vector(m_raw[0], m_bf[0])
+        rectify(0, 0, 0)
+        scores(0, 0, 3)
+        scores(1, 0, 1)
+        scores(1, 0, 2)
+        rectify(0, 0, 1)
+        scores(0, 1, 0)
+        rectify(0, 0, 2)
+        scores(0, 1, 1)
+        rectify(0, 0, 3)
+        rectify(1, 0, 0)
+        scores(1, 0, 3)
+        scores(0, 1, 2)
+        rectify(1, 0, 1)
+        scores(1, 1, 0)
+        rectify(1, 0, 2)
+        scores(1, 1, 1)
+        rectify(1, 0, 3)
+        scores(1, 1, 2)
+        square_vector(0, 0)
+        pack_values(0)
+        apply_mask(0, 0)
+        pack_values(1)
+        quantize_w(0, 0)
+        quantize(v_codes[:], v_scales[:], v_bf[:].rearrange("p h n -> p (h n)"))
+        square_scalar(1, 0)
+        rectify(0, 1, 0)
+        scores(0, 1, 3)
+        values(0, 0)
+        for r in range(1, 4):
+            rectify(0, 1, r)
+        apply_mask(1, 0)
+        pack_vector(m_raw[1], m_bf[1])
+        quantize_w(1, 0)
+        rectify(1, 1, 0)
+        scores(1, 1, 3)
+        values(1, 0)
+        for r in range(1, 4):
+            rectify(1, 1, r)
+        denominator(0, 0)
+        square_vector(0, 1)
+        invert(0, 0)
+        denominator(1, 0)
+        square_scalar(1, 1)
+        apply_mask(0, 1)
+        invert(1, 0)
+        finish(0, 0)
+        quantize_w(0, 1)
+        values(0, 1)
+        apply_mask(1, 1)
+        denominator(0, 1)
+        finish(1, 0)
+        quantize_w(1, 1)
+        values(1, 1)
+        invert(0, 1)
+        finish(0, 1)
+        denominator(1, 1)
+        invert(1, 1)
+        finish(1, 1)

@@ -18,9 +18,12 @@ PACK = 4
 ROWS = D // PACK
 HALF = NQ // 2
 QT = 128
-SCORE_BANKS = 3
+SCORE_BANKS = 2
 K_SPLIT = 88
 Q_SPLIT = 176
+SQ_SPLIT = 192
+VRUN = 2
+SRUN = 1
 
 
 def tile_rows_a_relu2_kb_mask_kernel(tc, qT, kT, t, v, kb, mask, out):
@@ -37,19 +40,17 @@ def tile_rows_a_relu2_kb_mask_kernel(tc, qT, kT, t, v, kb, mask, out):
         kb_sb = tile("kb_sb", [P, PACK], F32)
         k_raw = tile("k_raw", [P, PACK, N], F32)
         q_raw = [tile("q_raw%d" % u, [P, PACK, HALF], F32) for u in range(2)]
-        m_raw = [tile("m_raw%d" % u, [P, PACK, HALF], F32) for u in range(2)]
+        m_raw = tile("m_raw", [P, PACK, NQ], F32)
         v_raw = tile("v_raw", [P, H, PACK * E], F32)
 
         nc.scalar.dma_start(out=t_sb[:], in_=t.rearrange("(p r) o -> p (r o)", r=PACK))
         nc.scalar.dma_start(out=kb_sb[:], in_=kb.rearrange("(p r) o -> p (r o)", r=PACK))
         q_rows = qT.rearrange("h (p j) n -> (h p) j n", j=PACK)
-        m_rows = mask.rearrange("(p r) n -> p r n", r=PACK)
         nc.sync.dma_start(out=k_raw[:], in_=kT.rearrange("h (p j) n -> (h p) j n", j=PACK))
         nc.sync.dma_start(out=q_raw[0][:], in_=q_rows[:, :, 0:HALF])
         nc.sync.dma_start(out=q_raw[1][:], in_=q_rows[:, :, HALF:NQ])
-        nc.sync.dma_start(out=m_raw[0][:], in_=m_rows[:, :, 0:HALF])
         nc.sync.dma_start(out=v_raw[:], in_=v.rearrange("h (p j) e -> p h (j e)", j=PACK))
-        nc.sync.dma_start(out=m_raw[1][:], in_=m_rows[:, :, HALF:NQ])
+        nc.sync.dma_start(out=m_raw[:], in_=mask.rearrange("(p r) n -> p r n", r=PACK))
 
         t_sign = tile("t_sign", [P, PACK], F32)
         t_abs = tile("t_abs", [P, PACK], F32)
@@ -63,104 +64,96 @@ def tile_rows_a_relu2_kb_mask_kernel(tc, qT, kT, t, v, kb, mask, out):
         )
         nc.scalar.activation(out=half_root[:], in_=t_abs[:], func=ACT.Sqrt, scale=0.25)
         nc.scalar.activation(out=t_sign[:], in_=t_sb[:], func=ACT.Sign)
-        nc.vector.reciprocal(out=inv_half_root[:], in_=half_root[:])
-        nc.vector.scalar_tensor_tensor(
-            out=newton[:], in0=t_abs[:], scalar=0.25, in1=inv_half_root[:], op0=ALU.mult, op1=ALU.mult
-        )
-
-        k_bf = tile("k_bf", [P, PACK, P * PACK], BF16)
-        k_codes = tile("k_codes", [P, N], U32)
-        k_scales = tile("k_scales", [P, N], U8)
-        k_src = k_raw[:].rearrange("p j (m r) -> p m j r", r=PACK)
-        k_dst = k_bf[:].rearrange("p r (m j) -> p m j r", j=PACK)
-        nc.vector.tensor_copy(out=k_dst[:, 0:K_SPLIT], in_=k_src[:, 0:K_SPLIT])
-        nc.scalar.copy(out=k_dst[:, K_SPLIT:P], in_=k_src[:, K_SPLIT:P])
-        nc.vector.tensor_tensor(out=root[:], in0=newton[:], in1=half_root[:], op=ALU.add)
-        nc.vector.quantize_mx(
-            out=k_codes[:].bitcast(FP8X4), scales=k_scales[:], in_=k_bf[:].rearrange("p r n -> p (r n)")
-        )
-        nc.vector.tensor_tensor(out=kb_root[:], in0=kb_sb[:], in1=root[:], op=ALU.mult)
-
-        def by_fours(raw, packed):
-            src = raw.rearrange("p j (c i) -> p c j i", i=PACK)
-            dst = packed.rearrange("p (c i j) -> p c j i", i=PACK, j=PACK)
-            return src, dst
-
-        q_bf = [tile("q_bf%d" % u, [P, HALF * PACK], BF16) for u in range(2)]
-        q_codes = [tile("q_codes%d" % u, [P, HALF], U32) for u in range(2)]
-        q_scales = [tile("q_scales%d" % u, [P, HALF], U8) for u in range(2)]
-        m_bf = [tile("m_bf%d" % u, [P, HALF * PACK], BF16) for u in range(2)]
-        v_bf = tile("v_bf", [P, H, E * PACK], BF16)
-        v_codes = tile("v_codes", [P, H * E], U32)
-        v_scales = tile("v_scales", [P, H * E], U8)
 
         def quantize(codes, scales, packed):
             nc.vector.quantize_mx(out=codes.bitcast(FP8X4), scales=scales, in_=packed)
 
-        score_banks = [[ps.tile([P, HALF], F32, name="score%d_%d" % (h, b)) for b in range(SCORE_BANKS)] for h in range(H)]
-        y_banks = [ps.tile([P, 2 * HALF], F32, name="y%d" % b) for b in range(2)]
-        relu = {}
-        w_sq = {}
-        w_bf = {}
-        w_codes = {}
-        w_scales = {}
-        den = {}
-        inv = {}
-        res = {}
-        for u in range(2):
-            for h in range(H):
-                s = "%d%d" % (h, u)
-                relu[h, u] = tile("relu" + s, [P, PACK, HALF], F32)
-                w_sq[h, u] = tile("w_sq" + s, [P, HALF * PACK], BF16)
-                w_bf[h, u] = tile("w_bf" + s, [P, HALF * PACK], BF16)
-                w_codes[h, u] = tile("w_codes" + s, [P, HALF], U32)
-                w_scales[h, u] = tile("w_scales" + s, [P, HALF], U8)
-                den[h, u] = tile("den" + s, [P, 2], F32)
-                inv[h, u] = tile("inv" + s, [P, 2], F32)
-                res[h, u] = tile("res" + s, [P, 2, E], F32)
+        def vector_views(raw, packed, c0, c1):
+            src = raw[:, :, c0:c1].rearrange("p j (c i) -> p c j i", i=VRUN)
+            dst = packed[:, PACK * c0 : PACK * c1].rearrange("p (c i j) -> p c j i", i=VRUN, j=PACK)
+            return src, dst
 
-        def scores(h, u, r):
-            bank = score_banks[h][(PACK * u + r) % SCORE_BANKS]
+        def scalar_views(raw, packed, c0, c1):
+            src = raw[:, :, c0:c1].rearrange("p j (c i) -> p c j i", i=SRUN)
+            dst = packed[:, PACK * c0 : PACK * c1].rearrange("p (c i j) -> p c j i", i=SRUN, j=PACK)
+            return src, dst
+
+        k_bf = tile("k_bf", [P, PACK, P * PACK], BF16)
+        k_codes = tile("k_codes", [P, N], U32)
+        k_scales = tile("k_scales", [P, N], U8)
+        q_bf = [tile("q_bf%d" % u, [P, HALF * PACK], BF16) for u in range(2)]
+        q_codes = [tile("q_codes%d" % u, [P, HALF], U32) for u in range(2)]
+        q_scales = [tile("q_scales%d" % u, [P, HALF], U8) for u in range(2)]
+        m_bf = tile("m_bf", [P, NQ * PACK], BF16)
+        v_bf = tile("v_bf", [P, H, E * PACK], BF16)
+        v_codes = tile("v_codes", [P, H * E], U32)
+        v_scales = tile("v_scales", [P, H * E], U8)
+
+        score_banks = [[ps.tile([P, HALF], F32, name="score%d_%d" % (h, b)) for b in range(SCORE_BANKS)] for h in range(H)]
+        y_first = ps.tile([P, H, 2, E], F32, name="y_first")
+        y_third = ps.tile([P, 2, E], F32, name="y_third")
+        y_last = [ps.tile([P, 1, E], F32, name="y_last%d" % c) for c in range(2)]
+        units = [(h, u) for u in range(2) for h in range(H)]
+        relu = {hu: tile("relu%d%d" % hu, [P, PACK, HALF], F32) for hu in units}
+        w_sq = {hu: tile("w_sq%d%d" % hu, [P, HALF * PACK], BF16) for hu in units}
+        w_bf = {hu: tile("w_bf%d%d" % hu, [P, HALF * PACK], BF16) for hu in units}
+        w_codes = {hu: tile("w_codes%d%d" % hu, [P, HALF], U32) for hu in units}
+        w_scales = {hu: tile("w_scales%d%d" % hu, [P, HALF], U8) for hu in units}
+        res = {hu: tile("res%d%d" % hu, [P, 2, E], F32) for hu in units}
+
+        def scores(h, n):
+            u, r = divmod(n, PACK)
             rows = slice(ROWS * h, ROWS * (h + 1))
             toks = slice(P * r, P * (r + 1))
-            for c in range(2):
-                cols = slice(QT * c, QT * (c + 1))
-                nc.tensor.matmul_mx(
-                    out=bank[:, cols],
+            return [
+                dict(
+                    out=score_banks[h][n % SCORE_BANKS][:, QT * c : QT * (c + 1)],
                     lhsT=k_codes[rows, toks].bitcast(FP8X4),
                     lhsT_scale=k_scales[rows, toks],
-                    rhs=q_codes[u][rows, cols].bitcast(FP8X4),
-                    rhs_scale=q_scales[u][rows, cols],
+                    rhs=q_codes[u][rows, QT * c : QT * (c + 1)].bitcast(FP8X4),
+                    rhs_scale=q_scales[u][rows, QT * c : QT * (c + 1)],
                     start=True,
                     stop=True,
                 )
+                for c in range(2)
+            ]
 
-        def rectify(h, u, r):
-            bank = score_banks[h][(PACK * u + r) % SCORE_BANKS]
-            nc.scalar.activation(
-                out=relu[h, u][:, r, :], in_=bank[:], func=ACT.Relu, scale=root[:, r : r + 1], bias=kb_root[:, r : r + 1]
-            )
+        def rectify_half(u):
+            for r in range(PACK):
+                n = PACK * u + r
+                for h in range(H):
+                    nc.scalar.activation(
+                        out=relu[h, u][:, r, :],
+                        in_=score_banks[h][n % SCORE_BANKS][:],
+                        func=ACT.Relu,
+                        scale=root[:, r : r + 1],
+                        bias=kb_root[:, r : r + 1],
+                    )
+                    if n + SCORE_BANKS < 2 * PACK:
+                        for call in scores(h, n + SCORE_BANKS):
+                            nc.tensor.matmul_mx(**call)
 
-        def square_scalar(h, u):
-            src, dst = by_fours(relu[h, u][:], w_sq[h, u][:])
+        def square_scalar(h, u, c0, c1):
+            src, dst = scalar_views(relu[h, u], w_sq[h, u], c0, c1)
             nc.scalar.activation(out=dst, in_=src, func=ACT.Square)
 
-        def square_vector(h, u):
-            src, dst = by_fours(relu[h, u][:], w_sq[h, u][:])
+        def square_vector(h, u, c0, c1):
+            src, dst = vector_views(relu[h, u], w_sq[h, u], c0, c1)
             nc.vector.tensor_tensor(out=dst, in0=src, in1=src, op=ALU.mult)
 
-        def apply_mask(h, u):
-            nc.vector.tensor_tensor(out=w_bf[h, u][:], in0=w_sq[h, u][:], in1=m_bf[u][:], op=ALU.mult)
+        def apply_mask(h, u, c0, c1):
+            part = slice(c0 * PACK, c1 * PACK)
+            seen = m_bf[:, (HALF * u + c0) * PACK : (HALF * u + c1) * PACK]
+            nc.vector.tensor_tensor(out=w_bf[h, u][:, part], in0=w_sq[h, u][:, part], in1=seen, op=ALU.mult)
 
-        def quantize_w(h, u):
-            quantize(w_codes[h, u][:], w_scales[h, u][:], w_bf[h, u][:])
-
-        def values(h, u):
-            for c in range(2):
-                cols = slice(QT * c, QT * (c + 1))
-                feats = slice(E * h, E * (h + 1))
+        def values(h, u, c0, y):
+            c1 = c0 + QT * y.shape[1]
+            quantize(w_codes[h, u][:, c0:c1], w_scales[h, u][:, c0:c1], w_bf[h, u][:, c0 * PACK : c1 * PACK])
+            feats = slice(E * h, E * (h + 1))
+            for c in range(y.shape[1]):
+                cols = slice(c0 + QT * c, c0 + QT * (c + 1))
                 nc.tensor.matmul_mx(
-                    out=y_banks[h][:, HALF * u + E * c : HALF * u + E * (c + 1)],
+                    out=y[:, c, :],
                     lhsT=w_codes[h, u][:, cols].bitcast(FP8X4),
                     lhsT_scale=w_scales[h, u][:, cols],
                     rhs=v_codes[:, feats].bitcast(FP8X4),
@@ -169,100 +162,96 @@ def tile_rows_a_relu2_kb_mask_kernel(tc, qT, kT, t, v, kb, mask, out):
                     stop=True,
                 )
 
-        def y_view(h, u):
-            return y_banks[h][:, HALF * u : HALF * (u + 1)].rearrange("p (c e) -> p c e", c=2)
+        def denominator(name, y):
+            den = tile("den_" + name, [P, y.shape[1]], F32)
+            nc.vector.tensor_scalar(out=den[:], in0=y[:, :, E - 1], scalar1=1.0, scalar2=None, op0=ALU.add)
+            return den
 
-        def denominator(h, u):
-            nc.vector.tensor_scalar(
-                out=den[h, u][:], in0=y_view(h, u)[:, :, E - 1], scalar1=1.0, scalar2=None, op0=ALU.add
-            )
+        def invert(name, den):
+            inv = tile("inv_" + name, [P, den.shape[1]], F32)
+            nc.vector.reciprocal(out=inv[:], in_=den[:])
+            return inv
 
-        def invert(h, u):
-            nc.vector.reciprocal(out=inv[h, u][:], in_=den[h, u][:])
+        def store(h, u, c0, c1):
+            rows = out[h, HALF * u + QT * c0 : HALF * u + QT * c1, :]
+            nc.sync.dma_start(out=rows.rearrange("(c p) e -> p c e", p=P), in_=res[h, u][:, c0:c1, :])
 
-        def finish(h, u):
+        def finish_scalar(h, u, y, inv):
             for c in range(2):
-                nc.scalar.activation(
-                    out=res[h, u][:, c, :], in_=y_view(h, u)[:, c, :], func=ACT.Copy, scale=inv[h, u][:, c : c + 1]
-                )
-            nc.sync.dma_start(
-                out=out[h, HALF * u : HALF * (u + 1), :].rearrange("(c p) e -> p c e", p=P), in_=res[h, u][:]
-            )
+                nc.scalar.activation(out=res[h, u][:, c, :], in_=y[:, c, :], func=ACT.Copy, scale=inv[:, c : c + 1])
+            store(h, u, 0, 2)
+
+        def finish_vector(h, u, c, y, inv):
+            nc.vector.tensor_scalar(out=res[h, u][:, c, :], in0=y[:, 0, :], scalar1=inv[:, 0:1], scalar2=None, op0=ALU.mult)
+            store(h, u, c, c + 1)
 
         def pack_values(h):
-            src, dst = by_fours(v_raw[:, h, :].rearrange("p (j e) -> p j e", j=PACK), v_bf[:, h, :])
-            sign = t_sign[:].unsqueeze(1).unsqueeze(3).to_broadcast([P, E // PACK, PACK, PACK])
+            src, dst = vector_views(v_raw[:, h, :].rearrange("p (j e) -> p j e", j=PACK), v_bf[:, h, :], 0, E)
+            sign = t_sign[:].unsqueeze(1).unsqueeze(3).to_broadcast([P, E // VRUN, PACK, VRUN])
             nc.vector.tensor_tensor(out=dst, in0=src, in1=sign, op=ALU.mult)
 
-        def pack_vector(raw, packed):
-            src, dst = by_fours(raw[:], packed[:])
+        def pack_vector(raw, packed, c0, c1):
+            src, dst = vector_views(raw, packed, c0, c1)
             nc.vector.tensor_copy(out=dst, in_=src)
 
-        src, dst = by_fours(q_raw[0][:], q_bf[0][:])
-        nc.vector.tensor_copy(out=dst[:, 0 : Q_SPLIT // PACK], in_=src[:, 0 : Q_SPLIT // PACK])
-        nc.scalar.copy(out=dst[:, Q_SPLIT // PACK :], in_=src[:, Q_SPLIT // PACK :])
+        def quantize_keys(r0, r1):
+            toks = slice(P * r0, P * r1)
+            quantize(k_codes[:, toks], k_scales[:, toks], k_bf[:, r0:r1, :].rearrange("p r n -> p (r n)"))
+
+        k_src = k_raw[:].rearrange("p j (m r) -> p m r j", r=PACK)
+        k_dst = k_bf[:].rearrange("p r (m j) -> p m r j", j=PACK)
+        nc.vector.tensor_copy(out=k_dst[:, 0:K_SPLIT], in_=k_src[:, 0:K_SPLIT])
+        nc.scalar.copy(out=k_dst[:, K_SPLIT:P], in_=k_src[:, K_SPLIT:P])
+        nc.vector.reciprocal(out=inv_half_root[:], in_=half_root[:])
+        quantize_keys(0, 2)
+        nc.vector.scalar_tensor_tensor(
+            out=newton[:], in0=t_abs[:], scalar=0.25, in1=inv_half_root[:], op0=ALU.mult, op1=ALU.mult
+        )
+        pack_vector(q_raw[0], q_bf[0], 0, Q_SPLIT)
+        src, dst = scalar_views(q_raw[0], q_bf[0], Q_SPLIT, HALF)
+        nc.scalar.copy(out=dst, in_=src)
+        nc.vector.tensor_tensor(out=root[:], in0=newton[:], in1=half_root[:], op=ALU.add)
         quantize(q_codes[0][:], q_scales[0][:], q_bf[0][:])
-        pack_vector(q_raw[1], q_bf[1])
-        for r in range(3):
-            scores(0, 0, r)
-        scores(1, 0, 0)
+        nc.vector.tensor_tensor(out=kb_root[:], in0=kb_sb[:], in1=root[:], op=ALU.mult)
+        quantize_keys(2, 4)
+        pack_vector(q_raw[1], q_bf[1], 0, HALF)
+        for n in range(SCORE_BANKS):
+            for pair in zip(scores(0, n), scores(1, n)):
+                for call in pair:
+                    nc.tensor.matmul_mx(**call)
         quantize(q_codes[1][:], q_scales[1][:], q_bf[1][:])
-        pack_vector(m_raw[0], m_bf[0])
-        rectify(0, 0, 0)
-        scores(0, 0, 3)
-        scores(1, 0, 1)
-        scores(1, 0, 2)
-        rectify(0, 0, 1)
-        scores(0, 1, 0)
-        rectify(0, 0, 2)
-        scores(0, 1, 1)
-        rectify(0, 0, 3)
-        rectify(1, 0, 0)
-        scores(1, 0, 3)
-        scores(0, 1, 2)
-        rectify(1, 0, 1)
-        scores(1, 1, 0)
-        rectify(1, 0, 2)
-        scores(1, 1, 1)
-        rectify(1, 0, 3)
-        scores(1, 1, 2)
-        square_vector(0, 0)
         pack_values(0)
-        apply_mask(0, 0)
         pack_values(1)
-        quantize_w(0, 0)
+        rectify_half(0)
         quantize(v_codes[:], v_scales[:], v_bf[:].rearrange("p h n -> p (h n)"))
-        square_scalar(1, 0)
-        rectify(0, 1, 0)
-        scores(0, 1, 3)
-        values(0, 0)
-        for r in range(1, 4):
-            rectify(0, 1, r)
-        apply_mask(1, 0)
-        pack_vector(m_raw[1], m_bf[1])
-        quantize_w(1, 0)
-        rectify(1, 1, 0)
-        scores(1, 1, 3)
-        values(1, 0)
-        for r in range(1, 4):
-            rectify(1, 1, r)
-        denominator(0, 0)
-        square_vector(0, 1)
-        invert(0, 0)
-        denominator(1, 0)
-        square_scalar(1, 1)
-        apply_mask(0, 1)
-        invert(1, 0)
-        finish(0, 0)
-        quantize_w(0, 1)
-        values(0, 1)
-        apply_mask(1, 1)
-        denominator(0, 1)
-        finish(1, 0)
-        quantize_w(1, 1)
-        values(1, 1)
-        invert(0, 1)
-        finish(0, 1)
-        denominator(1, 1)
-        invert(1, 1)
-        finish(1, 1)
+        square_vector(0, 0, 0, HALF)
+        pack_vector(m_raw, m_bf, 0, NQ)
+        square_vector(1, 0, 0, SQ_SPLIT)
+        square_scalar(1, 0, SQ_SPLIT, HALF)
+        rectify_half(1)
+        apply_mask(0, 0, 0, HALF)
+        apply_mask(1, 0, 0, HALF)
+        square_scalar(0, 1, 0, HALF)
+        values(0, 0, 0, y_first[:, 0])
+        values(1, 0, 0, y_first[:, 1])
+        square_scalar(1, 1, 0, QT)
+        square_scalar(1, 1, QT, HALF)
+        apply_mask(0, 1, 0, HALF)
+        den_first = denominator("first", y_first[:].rearrange("p h c e -> p (h c) e"))
+        apply_mask(1, 1, 0, QT)
+        inv_first = invert("first", den_first)
+        values(0, 1, 0, y_third[:])
+        values(1, 1, 0, y_last[0][:])
+        apply_mask(1, 1, QT, HALF)
+        finish_scalar(0, 0, y_first[:, 0], inv_first[:, 0:2])
+        finish_scalar(1, 0, y_first[:, 1], inv_first[:, 2:4])
+        den_third = denominator("third", y_third[:])
+        values(1, 1, QT, y_last[1][:])
+        den_last0 = denominator("last0", y_last[0][:])
+        inv_third = invert("third", den_third)
+        inv_last0 = invert("last0", den_last0)
+        finish_scalar(0, 1, y_third[:], inv_third)
+        den_last1 = denominator("last1", y_last[1][:])
+        finish_vector(1, 1, 0, y_last[0][:], inv_last0)
+        inv_last1 = invert("last1", den_last1)
+        finish_vector(1, 1, 1, y_last[1][:], inv_last1)

from contextlib import ExitStack

import concourse.mybir as mybir

H, D, NQ, N, E = 2, 256, 512, 512, 128
FLOPS = 2 * H * N * NQ * D + 2 * H * NQ * N * E

F32 = mybir.dt.float32
BF16 = mybir.dt.bfloat16
U32 = mybir.dt.uint32
U8 = mybir.dt.uint8
FP8X4 = mybir.dt.float8_e4m3fn_x4
ACT = mybir.ActivationFunctionType
ALU = mybir.AluOpType

P = 128
PACK = 4
ROWS = D // PACK
HALF = NQ // 2
QT = 128
SCORE_BANKS = 2
K_SPLIT = 88
Q_SPLIT = 176
SQ_SPLIT = 192
VRUN = 2
SRUN = 1


def tile_rows_a_relu2_kb_mask_kernel(tc, qT, kT, t, v, kb, mask, out):
    nc = tc.nc
    with ExitStack() as ctx:
        sb = ctx.enter_context(tc.tile_pool(name="sb", bufs=1))
        ps = ctx.enter_context(tc.psum_pool(name="ps", bufs=1))
        ctx.enter_context(tc.manual_schedule())

        def tile(name, shape, dtype):
            return sb.tile(shape, dtype, name=name, align_bytes=64)

        t_sb = tile("t_sb", [P, PACK], F32)
        kb_sb = tile("kb_sb", [P, PACK], F32)
        k_raw = tile("k_raw", [P, PACK, N], F32)
        q_raw = [tile("q_raw%d" % u, [P, PACK, HALF], F32) for u in range(2)]
        m_raw = tile("m_raw", [P, PACK, NQ], F32)
        v_raw = tile("v_raw", [P, H, PACK * E], F32)

        nc.scalar.dma_start(out=t_sb[:], in_=t.rearrange("(p r) o -> p (r o)", r=PACK))
        nc.scalar.dma_start(out=kb_sb[:], in_=kb.rearrange("(p r) o -> p (r o)", r=PACK))
        q_rows = qT.rearrange("h (p j) n -> (h p) j n", j=PACK)
        nc.sync.dma_start(out=k_raw[:], in_=kT.rearrange("h (p j) n -> (h p) j n", j=PACK))
        nc.sync.dma_start(out=q_raw[0][:], in_=q_rows[:, :, 0:HALF])
        nc.sync.dma_start(out=q_raw[1][:], in_=q_rows[:, :, HALF:NQ])
        nc.sync.dma_start(out=v_raw[:], in_=v.rearrange("h (p j) e -> p h (j e)", j=PACK))
        nc.sync.dma_start(out=m_raw[:], in_=mask.rearrange("(p r) n -> p r n", r=PACK))

        t_sign = tile("t_sign", [P, PACK], F32)
        t_abs = tile("t_abs", [P, PACK], F32)
        half_root = tile("half_root", [P, PACK], F32)
        inv_half_root = tile("inv_half_root", [P, PACK], F32)
        newton = tile("newton", [P, PACK], F32)
        root = tile("root", [P, PACK], F32)
        kb_root = tile("kb_root", [P, PACK], F32)
        nc.vector.scalar_tensor_tensor(
            out=t_abs[:], in0=t_sb[:], scalar=-1.0, in1=t_sb[:], op0=ALU.mult, op1=ALU.max
        )
        nc.scalar.activation(out=half_root[:], in_=t_abs[:], func=ACT.Sqrt, scale=0.25)
        nc.scalar.activation(out=t_sign[:], in_=t_sb[:], func=ACT.Sign)

        def quantize(codes, scales, packed):
            nc.vector.quantize_mx(out=codes.bitcast(FP8X4), scales=scales, in_=packed)

        def vector_views(raw, packed, c0, c1):
            src = raw[:, :, c0:c1].rearrange("p j (c i) -> p c j i", i=VRUN)
            dst = packed[:, PACK * c0 : PACK * c1].rearrange("p (c i j) -> p c j i", i=VRUN, j=PACK)
            return src, dst

        def scalar_views(raw, packed, c0, c1):
            src = raw[:, :, c0:c1].rearrange("p j (c i) -> p c j i", i=SRUN)
            dst = packed[:, PACK * c0 : PACK * c1].rearrange("p (c i j) -> p c j i", i=SRUN, j=PACK)
            return src, dst

        k_bf = tile("k_bf", [P, PACK, P * PACK], BF16)
        k_codes = tile("k_codes", [P, N], U32)
        k_scales = tile("k_scales", [P, N], U8)
        q_bf = [tile("q_bf%d" % u, [P, HALF * PACK], BF16) for u in range(2)]
        q_codes = [tile("q_codes%d" % u, [P, HALF], U32) for u in range(2)]
        q_scales = [tile("q_scales%d" % u, [P, HALF], U8) for u in range(2)]
        m_bf = tile("m_bf", [P, NQ * PACK], BF16)
        v_bf = tile("v_bf", [P, H, E * PACK], BF16)
        v_codes = tile("v_codes", [P, H * E], U32)
        v_scales = tile("v_scales", [P, H * E], U8)

        score_banks = [[ps.tile([P, HALF], F32, name="score%d_%d" % (h, b)) for b in range(SCORE_BANKS)] for h in range(H)]
        y_first = ps.tile([P, H, 2, E], F32, name="y_first")
        y_third = ps.tile([P, 2, E], F32, name="y_third")
        y_last = [ps.tile([P, 1, E], F32, name="y_last%d" % c) for c in range(2)]
        units = [(h, u) for u in range(2) for h in range(H)]
        relu = {hu: tile("relu%d%d" % hu, [P, PACK, HALF], F32) for hu in units}
        w_sq = {hu: tile("w_sq%d%d" % hu, [P, HALF * PACK], BF16) for hu in units}
        w_bf = {hu: tile("w_bf%d%d" % hu, [P, HALF * PACK], BF16) for hu in units}
        w_codes = {hu: tile("w_codes%d%d" % hu, [P, HALF], U32) for hu in units}
        w_scales = {hu: tile("w_scales%d%d" % hu, [P, HALF], U8) for hu in units}
        res = {hu: tile("res%d%d" % hu, [P, 2, E], F32) for hu in units}

        def scores(h, n):
            u, r = divmod(n, PACK)
            rows = slice(ROWS * h, ROWS * (h + 1))
            toks = slice(P * r, P * (r + 1))
            return [
                dict(
                    out=score_banks[h][n % SCORE_BANKS][:, QT * c : QT * (c + 1)],
                    lhsT=k_codes[rows, toks].bitcast(FP8X4),
                    lhsT_scale=k_scales[rows, toks],
                    rhs=q_codes[u][rows, QT * c : QT * (c + 1)].bitcast(FP8X4),
                    rhs_scale=q_scales[u][rows, QT * c : QT * (c + 1)],
                    start=True,
                    stop=True,
                )
                for c in range(2)
            ]

        def rectify_half(u):
            for r in range(PACK):
                n = PACK * u + r
                for h in range(H):
                    nc.scalar.activation(
                        out=relu[h, u][:, r, :],
                        in_=score_banks[h][n % SCORE_BANKS][:],
                        func=ACT.Relu,
                        scale=root[:, r : r + 1],
                        bias=kb_root[:, r : r + 1],
                    )
                    if n + SCORE_BANKS < 2 * PACK:
                        for call in scores(h, n + SCORE_BANKS):
                            nc.tensor.matmul_mx(**call)

        def square_scalar(h, u, c0, c1):
            src, dst = scalar_views(relu[h, u], w_sq[h, u], c0, c1)
            nc.scalar.activation(out=dst, in_=src, func=ACT.Square)

        def square_vector(h, u, c0, c1):
            src, dst = vector_views(relu[h, u], w_sq[h, u], c0, c1)
            nc.vector.tensor_tensor(out=dst, in0=src, in1=src, op=ALU.mult)

        def apply_mask(h, u, c0, c1):
            part = slice(c0 * PACK, c1 * PACK)
            seen = m_bf[:, (HALF * u + c0) * PACK : (HALF * u + c1) * PACK]
            nc.vector.tensor_tensor(out=w_bf[h, u][:, part], in0=w_sq[h, u][:, part], in1=seen, op=ALU.mult)

        def values(h, u, c0, y):
            c1 = c0 + QT * y.shape[1]
            quantize(w_codes[h, u][:, c0:c1], w_scales[h, u][:, c0:c1], w_bf[h, u][:, c0 * PACK : c1 * PACK])
            feats = slice(E * h, E * (h + 1))
            for c in range(y.shape[1]):
                cols = slice(c0 + QT * c, c0 + QT * (c + 1))
                nc.tensor.matmul_mx(
                    out=y[:, c, :],
                    lhsT=w_codes[h, u][:, cols].bitcast(FP8X4),
                    lhsT_scale=w_scales[h, u][:, cols],
                    rhs=v_codes[:, feats].bitcast(FP8X4),
                    rhs_scale=v_scales[:, feats],
                    start=True,
                    stop=True,
                )

        def denominator(name, y):
            den = tile("den_" + name, [P, y.shape[1]], F32)
            nc.vector.tensor_scalar(out=den[:], in0=y[:, :, E - 1], scalar1=1.0, scalar2=None, op0=ALU.add)
            return den

        def invert(name, den):
            inv = tile("inv_" + name, [P, den.shape[1]], F32)
            nc.vector.reciprocal(out=inv[:], in_=den[:])
            return inv

        def store(h, u, c0, c1):
            rows = out[h, HALF * u + QT * c0 : HALF * u + QT * c1, :]
            nc.sync.dma_start(out=rows.rearrange("(c p) e -> p c e", p=P), in_=res[h, u][:, c0:c1, :])

        def finish_scalar(h, u, y, inv):
            for c in range(2):
                nc.scalar.activation(out=res[h, u][:, c, :], in_=y[:, c, :], func=ACT.Copy, scale=inv[:, c : c + 1])
            store(h, u, 0, 2)

        def finish_vector(h, u, c, y, inv):
            nc.vector.tensor_scalar(out=res[h, u][:, c, :], in0=y[:, 0, :], scalar1=inv[:, 0:1], scalar2=None, op0=ALU.mult)
            store(h, u, c, c + 1)

        def pack_values(h):
            src, dst = vector_views(v_raw[:, h, :].rearrange("p (j e) -> p j e", j=PACK), v_bf[:, h, :], 0, E)
            sign = t_sign[:].unsqueeze(1).unsqueeze(3).to_broadcast([P, E // VRUN, PACK, VRUN])
            nc.vector.tensor_tensor(out=dst, in0=src, in1=sign, op=ALU.mult)

        def pack_vector(raw, packed, c0, c1):
            src, dst = vector_views(raw, packed, c0, c1)
            nc.vector.tensor_copy(out=dst, in_=src)

        def quantize_keys(r0, r1):
            toks = slice(P * r0, P * r1)
            quantize(k_codes[:, toks], k_scales[:, toks], k_bf[:, r0:r1, :].rearrange("p r n -> p (r n)"))

        k_src = k_raw[:].rearrange("p j (m r) -> p m r j", r=PACK)
        k_dst = k_bf[:].rearrange("p r (m j) -> p m r j", j=PACK)
        nc.vector.tensor_copy(out=k_dst[:, 0:K_SPLIT], in_=k_src[:, 0:K_SPLIT])
        nc.scalar.copy(out=k_dst[:, K_SPLIT:P], in_=k_src[:, K_SPLIT:P])
        nc.vector.reciprocal(out=inv_half_root[:], in_=half_root[:])
        quantize_keys(0, 2)
        nc.vector.scalar_tensor_tensor(
            out=newton[:], in0=t_abs[:], scalar=0.25, in1=inv_half_root[:], op0=ALU.mult, op1=ALU.mult
        )
        pack_vector(q_raw[0], q_bf[0], 0, Q_SPLIT)
        src, dst = scalar_views(q_raw[0], q_bf[0], Q_SPLIT, HALF)
        nc.scalar.copy(out=dst, in_=src)
        nc.vector.tensor_tensor(out=root[:], in0=newton[:], in1=half_root[:], op=ALU.add)
        quantize(q_codes[0][:], q_scales[0][:], q_bf[0][:])
        nc.vector.tensor_tensor(out=kb_root[:], in0=kb_sb[:], in1=root[:], op=ALU.mult)
        quantize_keys(2, 4)
        pack_vector(q_raw[1], q_bf[1], 0, HALF)
        for n in range(SCORE_BANKS):
            for pair in zip(scores(0, n), scores(1, n)):
                for call in pair:
                    nc.tensor.matmul_mx(**call)
        quantize(q_codes[1][:], q_scales[1][:], q_bf[1][:])
        pack_values(0)
        pack_values(1)
        rectify_half(0)
        quantize(v_codes[:], v_scales[:], v_bf[:].rearrange("p h n -> p (h n)"))
        square_vector(0, 0, 0, HALF)
        pack_vector(m_raw, m_bf, 0, NQ)
        square_vector(1, 0, 0, SQ_SPLIT)
        square_scalar(1, 0, SQ_SPLIT, HALF)
        rectify_half(1)
        apply_mask(0, 0, 0, HALF)
        apply_mask(1, 0, 0, HALF)
        square_scalar(0, 1, 0, HALF)
        values(0, 0, 0, y_first[:, 0])
        values(1, 0, 0, y_first[:, 1])
        square_scalar(1, 1, 0, QT)
        square_scalar(1, 1, QT, HALF)
        apply_mask(0, 1, 0, HALF)
        den_first = denominator("first", y_first[:].rearrange("p h c e -> p (h c) e"))
        apply_mask(1, 1, 0, QT)
        inv_first = invert("first", den_first)
        values(0, 1, 0, y_third[:])
        values(1, 1, 0, y_last[0][:])
        apply_mask(1, 1, QT, HALF)
        finish_scalar(0, 0, y_first[:, 0], inv_first[:, 0:2])
        finish_scalar(1, 0, y_first[:, 1], inv_first[:, 2:4])
        den_third = denominator("third", y_third[:])
        values(1, 1, QT, y_last[1][:])
        den_last0 = denominator("last0", y_last[0][:])
        inv_third = invert("third", den_third)
        inv_last0 = invert("last0", den_last0)
        finish_scalar(0, 1, y_third[:], inv_third)
        den_last1 = denominator("last1", y_last[1][:])
        finish_vector(1, 1, 0, y_last[0][:], inv_last0)
        inv_last1 = invert("last1", den_last1)
        finish_vector(1, 1, 1, y_last[1][:], inv_last1)
